import numpy as np, ml_dtypes
CORES = [2,3,6,7,58,59,62,63,114,115,118,119]
N = 12
import mx_ref
NC, G = 128, 4
C = np.float32(0.00048828125)
BF = ml_dtypes.bfloat16
def cut(t, i, w=512):
    return t[:, w * i:w * i + w]
def tile(rs):
    return np.stack(rs, axis=2).reshape(128, -1).astype(BF)
def layer(w, X):
    out = []
    for i in range(G):
        for t in range(len(X)):
            p = mx_ref.matmul(mx_ref.quantize(cut(w, len(X) * i + t)), X[t])
            z = p if t == 0 else z + p
        out.append(z)
    return out
def gate(U, V):
    return [(np.maximum(u, 0) * v) * C for u, v in zip(U, V)]
def setup_inputs(rng):
    def f(*shape):
        return mx_ref.flush((rng.standard_normal(shape, dtype=np.float32) * np.exp2(rng.integers(-2, 3, shape[:-1] + (1,)))).astype(BF))
    return {"x": f(N, 128, 4 * NC), "u": f(N, 128, G * 512), "v": f(N, 128, G * 512), "w2": f(N, 128, 512)}
def setup_inputs_blocks(rng):
    d = setup_inputs(rng)
    for k in ("x", "u", "v", "w2"): d[k] = mx_ref.spread(d[k], rng, 4)
    return d
def setup_inputs_wide(rng):
    d = setup_inputs(rng)
    for k in ("x", "u", "v", "w2"): d[k] = mx_ref.flush((d[k].astype(np.float32) * np.exp2(rng.integers(-5, 6, (N, 1, 1))).astype(np.float32)).astype(BF))
    return d
def setup_inputs_zeros(rng):
    d = setup_inputs(rng); v = d["x"].reshape(N, 128, -1, 4).copy()
    v[np.broadcast_to((rng.random((N, 1, v.shape[2], 1)) < 0.33), v.shape)] = 0
    d["x"] = v.reshape(d["x"].shape)
    return d
def reference(x, u, v, w2):
    h = np.zeros((N, 128, 4 * NC), BF)
    for j in range(N):
        X = [mx_ref.quantize(x[j])]
        h[j] = tile(gate(layer(u[j], X), layer(v[j], X)))
    H = [mx_ref.quantize(h[j]) for j in range(N)]
    y = np.zeros((N, 128, N * NC), np.float32)
    for r in range(N):
        qw = mx_ref.quantize(w2[r])
        for j in range(N):
            y[r][:, NC * j:NC * j + NC] = mx_ref.matmul(qw, H[j])
    return {"y": y}

@@ -1,0 +1,188 @@
+from concourse.bass import DstId, RemoteDMATransfer
+from concourse.mybir import dt, AluOpType, ActivationFunctionType
+
+W = 128
+G = 4
+NT = 12
+C = 0.00048828125
+BANK = 512
+
+SCRATCH = {
+    "xb": ("sbuf", [128, 4 * W], "bfloat16"),
+    "ub": ("sbuf", [128, 4 * W * G], "bfloat16"),
+    "vb": ("sbuf", [128, 4 * W * G], "bfloat16"),
+    "wb": ("sbuf", [128, 4 * W], "bfloat16"),
+    "xq": ("sbuf", [128, W], "float8_e4m3fn_x4"), "xs": ("sbuf", [128, W], "uint8"),
+    "uq": ("sbuf", [128, W * G], "float8_e4m3fn_x4"), "us": ("sbuf", [128, W * G], "uint8"),
+    "vq": ("sbuf", [128, W * G], "float8_e4m3fn_x4"), "vs": ("sbuf", [128, W * G], "uint8"),
+    "wq": ("sbuf", [128, W], "float8_e4m3fn_x4"), "ws": ("sbuf", [128, W], "uint8"),
+    "ps": ("psum", [128, 8 * BANK], "float32"),
+    "rl": ("sbuf", [128, W * G], "float32"),
+    "hb": ("sbuf", [128, 4 * W], "bfloat16"),
+    "gq": ("sbuf", [128, W * NT], "float8_e4m3fn_x4"), "gs": ("sbuf", [128, W * NT], "uint8"),
+    "yb": ("sbuf", [128, W * NT], "float32"),
+}
+SEMAPHORES = (["lx", "lu", "lv0", "lv1", "lw", "qx", "hm", "qh", "qw", "on", "offp", "offc", "fw", "loc",
+               "mo0", "mo1", "co", "md0", "md1", "cg0", "cg1", "st"]
+              + ["%s%d" % (n, i) for n in ("qu", "qv", "mu", "mv", "rl") for i in range(G)]
+              + ["mf%d" % i for i in range(6)])
+
+
+def _count(mask):
+    return bin(mask).count("1")
+
+
+def rank_program(g, core, T, topo):
+    if T.rank_of(core) is None:
+        return
+    S = T.sem
+    vec, ten, act, syn = g.vector, g.tensor, g.scalar, g.sync
+
+    cores = list(T.cores)
+    chips = []
+    for c in cores:
+        if topo.chip(c) not in chips:
+            chips.append(topo.chip(c))
+    members = dict((ch, [c for c in cores if topo.chip(c) == ch]) for ch in chips)
+    here = topo.chip(core)
+    mine = members[here]
+    L = len(mine)
+    lane = mine.index(core)
+    peers = [mine[(lane + d) % L] for d in range(1, L)]
+    others = [ch for ch in chips if ch != here]
+    far = [members[ch][lane] for ch in others]
+    for d in far:
+        assert topo.may_write(core, d) and topo.die(d) == topo.die(core)
+
+    def slot(ch, o):
+        k = members[topo.chip(o)].index(o)
+        if topo.chip(o) == ch:
+            return W * k
+        rest = [c for c in chips if c != ch]
+        return W * (L + len(rest) * k + rest.index(topo.chip(o)))
+
+    m_off = topo.mask(core, far[0])
+    for d in far:
+        m_off &= topo.mask(core, d)
+    m_all = topo.mask(core, peers[0])
+    m_on = m_all & ~m_off
+    n_off, n_on, n_all = _count(m_off), _count(m_on), _count(m_all)
+
+    def send(codes, a, width, dsts, mask, sem):
+        def ap(c0):
+            if codes:
+                return T.gq[:, c0:c0 + width].bitcast(dt.uint8)
+            return T.gs[:, c0:c0 + width]
+        ids = [DstId(rid=topo.addr(d)[0], pnc=topo.addr(d)[1]) for d, _ in dsts]
+        g.remote_dma_fused([RemoteDMATransfer(dst_ids=ids, dma_engine_mask=mask, remote_sem=sem,
+                                              srcs=[ap(a)], dsts=[ap(c0) for _, c0 in dsts])], local_sem=S.loc)
+        return _count(mask)
+
+    H = 2 * W * G
+    syn.dma_start(T.xb[:], T.x[:]).then_inc(S.lx, 16)
+    act.dma_start(T.ub[:], T.u[:]).then_inc(S.lu, 16)
+    syn.dma_start(T.vb[:, 0:H], T.v[:, 0:H]).then_inc(S.lv0, 16)
+    act.dma_start(T.vb[:, H:2 * H], T.v[:, H:2 * H]).then_inc(S.lv1, 16)
+    syn.dma_start(T.wb[:], T.w2[:]).then_inc(S.lw, 16)
+
+    vec.wait_ge(S.lx, 16)
+    vec.quantize_mx(T.xq[:], T.xs[:], T.xb[:]).then_inc(S.qx, 1)
+    ten.wait_ge(S.qx, 1)
+    vec.wait_ge(S.lu, 16)
+    for i in range(G):
+        vec.quantize_mx(T.uq[:, W * i:W * i + W], T.us[:, W * i:W * i + W],
+                        T.ub[:, 4 * W * i:4 * W * i + 4 * W]).then_inc(S["qu%d" % i], 1)
+        ten.wait_ge(S["qu%d" % i], 1)
+        ten.matmul_mx(T.ps[:, BANK * i:BANK * i + W], T.uq[:, W * i:W * i + W], T.us[:, W * i:W * i + W],
+                      T.xq[:], T.xs[:], True, True).then_inc(S["mu%d" % i], 1)
+        act.wait_ge(S["mu%d" % i], 1)
+        act.activation(T.rl[:, W * i:W * i + W], T.ps[:, BANK * i:BANK * i + W], ActivationFunctionType.Relu,
+                       scale=C).then_inc(S["rl%d" % i], 1)
+    for half in range(2):
+        vec.wait_ge(S["lv%d" % half], 16)
+        two = (2 * half, 2 * half + 1)
+        for i in two:
+            vec.quantize_mx(T.vq[:, W * i:W * i + W], T.vs[:, W * i:W * i + W],
+                            T.vb[:, 4 * W * i:4 * W * i + 4 * W]).then_inc(S["qv%d" % i], 1)
+            ten.wait_ge(S["qv%d" % i], 1)
+            ten.matmul_mx(T.ps[:, BANK * (G + i):BANK * (G + i) + W], T.vq[:, W * i:W * i + W],
+                          T.vs[:, W * i:W * i + W], T.xq[:], T.xs[:], True, True).then_inc(S["mv%d" % i], 1)
+        for i in two:
+            vec.wait_ge(S["rl%d" % i], 1)
+            vec.wait_ge(S["mv%d" % i], 1)
+            vec.tensor_tensor(T.hb[:, i:4 * W:4], T.rl[:, W * i:W * i + W],
+                              T.ps[:, BANK * (G + i):BANK * (G + i) + W], AluOpType.mult).then_inc(S.hm, 1)
+    own = slot(here, core)
+    vec.wait_ge(S.hm, G)
+    vec.quantize_mx(T.gq[:, own:own + W], T.gs[:, own:own + W], T.hb[:]).then_inc(S.qh, 1)
+    vec.wait_ge(S.lw, 16)
+    vec.quantize_mx(T.wq[:], T.ws[:], T.wb[:]).then_inc(S.qw, 1)
+
+    left = 0
+    g.wait_ge(S.qh, 1)
+    off = [(d, slot(topo.chip(d), core)) for d in far]
+    left += send(False, own, W, off, m_off, S.offp)
+    left += send(True, own, W, off, m_off, S.offc)
+    near = [(p, own) for p in peers]
+    left += send(True, own, W, near, m_on, S.on)
+    left += send(False, own, W, near, m_on, S.on)
+    pair = slot(here, far[0])
+    assert [slot(here, d) for d in far] == [pair + W * s for s in range(len(far))]
+    wide = W * len(far)
+    on_to = [(p, pair) for p in peers]
+    g.wait_ge(S.offp, n_off * len(far))
+    left += send(False, pair, wide, on_to, m_all, S.fw)
+    g.wait_ge(S.offc, n_off * len(far))
+    left += send(True, pair, wide, on_to, m_all, S.fw)
+    g.wait_ge(S.loc, left)
+
+    def copy(k, out, in_):
+        if k == 0:
+            return vec.tensor_copy(out, in_)
+        return act.activation(out, in_, ActivationFunctionType.Copy)
+
+    def product(bank, col, n, sem):
+        ten.matmul_mx(T.ps[:, BANK * bank:BANK * bank + n], T.wq[:], T.ws[:], T.gq[:, col:col + n],
+                      T.gs[:, col:col + n], True, True).then_inc(sem, 1)
+
+    def ycol(o):
+        return W * T.rank_of(o)
+
+    ten.wait_ge(S.qw, 1)
+    ten.wait_ge(S.qh, 1)
+    for i in range(G):
+        ten.wait_ge(S["rl%d" % i], 1)
+    ten.wait_ge(S.hm, G)
+    assert [ycol(o) for o in mine] == [ycol(mine[0]) + W * k for k in range(L)]
+    ten.wait_ge(S.on, 2 * n_on * len(peers))
+    for k in range(2):
+        product(k, 2 * W * k, 2 * W, S["mo%d" % k])
+        (vec, act)[k].wait_ge(S["mo%d" % k], 1)
+        y0 = ycol(mine[0]) + 2 * W * k
+        copy(k, T.yb[:, y0:y0 + 2 * W], T.ps[:, BANK * k:BANK * k + 2 * W]).then_inc(S.co, 1)
+    syn.wait_ge(S.co, 2)
+    y0 = ycol(mine[0])
+    syn.dma_start(T.y[:, y0:y0 + L * W], T.yb[:, y0:y0 + L * W]).then_inc(S.st, 16)
+    ten.wait_ge(S.offp, n_off * len(far))
+    ten.wait_ge(S.offc, n_off * len(far))
+    for s, o in enumerate(far):
+        product(2 + s, slot(here, o), W, S["md%d" % s])
+        (vec, act)[s].wait_ge(S["md%d" % s], 1)
+        copy(s, T.yb[:, ycol(o):ycol(o) + W], T.ps[:, BANK * (2 + s):BANK * (2 + s) + W]).then_inc(S["cg%d" % s], 1)
+    ten.wait_ge(S.fw, 2 * n_all * len(peers))
+    ten.wait_ge(S.co, 2)
+    banks = [4, 5, 6, 7, 0, 1]
+    n = 0
+    for s, ch in enumerate(others):
+        for o in members[ch]:
+            if o in far:
+                continue
+            product(banks[n], slot(here, o), W, S["mf%d" % n])
+            (vec, act)[n % 2].wait_ge(S["mf%d" % n], 1)
+            copy(n % 2, T.yb[:, ycol(o):ycol(o) + W],
+                 T.ps[:, BANK * banks[n]:BANK * banks[n] + W]).then_inc(S["cg%d" % s], 1)
+            n += 1
+        y0 = ycol(members[ch][0])
+        syn.wait_ge(S["cg%d" % s], L)
+        syn.dma_start(T.y[:, y0:y0 + L * W], T.yb[:, y0:y0 + L * W]).then_inc(S.st, 16)
+    syn.wait_ge(S.st, 48)

@@ -22,10 +22,10 @@ SCRATCH = {
     "gq": ("sbuf", [128, W * NT], "float8_e4m3fn_x4"), "gs": ("sbuf", [128, W * NT], "uint8"),
     "yb": ("sbuf", [128, W * NT], "float32"),
 }
-SEMAPHORES = (["lx", "lu", "lv0", "lv1", "lw", "qx", "hm", "qh", "qw", "on", "offp", "offc", "fw", "loc",
-               "mo0", "mo1", "co", "md0", "md1", "cg0", "cg1", "st"]
-              + ["%s%d" % (n, i) for n in ("qu", "qv", "mu", "mv", "rl") for i in range(G)]
-              + ["mf%d" % i for i in range(6)])
+SEMAPHORES = (["lx", "lu", "lv0", "lv1", "lw", "qx", "hm", "qh", "qw", "on", "offp", "offc", "loc",
+               "mo0", "mo1", "co", "st"]
+              + ["%s%d" % (n, i) for n in ("qu", "qv", "mu", "mv", "rl", "fw", "cb") for i in range(G)]
+              + ["m%d%d" % (j, k) for j in range(4) for k in range(2)])
 
 
 def _count(mask):
@@ -43,23 +43,38 @@ def rank_program(g, core, T, topo):
     for c in cores:
         if topo.chip(c) not in chips:
             chips.append(topo.chip(c))
+    NCH = len(chips)
     members = dict((ch, [c for c in cores if topo.chip(c) == ch]) for ch in chips)
-    here = topo.chip(core)
+
+    def col(o):
+        return W * T.rank_of(o)
+
+    def on_die(ch, d):
+        return [c for c in members[ch] if topo.die(c) == d]
+
+    def sources(ch):
+        return [chips[(chips.index(ch) - s) % NCH] for s in range(1, NCH)]
+
+    def turn(c):
+        return on_die(topo.chip(c), topo.die(c)).index(c)
+
+    here, die = topo.chip(core), topo.die(core)
     mine = members[here]
     L = len(mine)
-    lane = mine.index(core)
-    peers = [mine[(lane + d) % L] for d in range(1, L)]
-    others = [ch for ch in chips if ch != here]
-    far = [members[ch][lane] for ch in others]
+    far = []
+    for s in range(1, NCH):
+        ch = chips[(chips.index(here) + s) % NCH]
+        far.append(on_die(ch, die)[sources(ch).index(here)])
     for d in far:
-        assert topo.may_write(core, d) and topo.die(d) == topo.die(core)
+        assert topo.may_write(core, d) and topo.die(d) == die
 
-    def slot(ch, o):
-        k = members[topo.chip(o)].index(o)
-        if topo.chip(o) == ch:
-            return W * k
-        rest = [c for c in chips if c != ch]
-        return W * (L + len(rest) * k + rest.index(topo.chip(o)))
+    def pair_of(c):
+        src = on_die(sources(topo.chip(c))[turn(c)], topo.die(c))
+        assert [col(o) for o in src] == [col(src[0]) + W * k for k in range(len(src))]
+        return col(src[0]), W * len(src), len(src)
+
+    peers = sorted([p for p in mine if p != core], key=lambda p: (turn(p) == turn(core), topo.die(p) != die))
+    givers = sorted([p for p in mine if p != core], key=lambda p: (turn(p), topo.die(p) != die))
 
     m_off = topo.mask(core, far[0])
     for d in far:
@@ -69,13 +84,13 @@ def rank_program(g, core, T, topo):
     n_off, n_on, n_all = _count(m_off), _count(m_on), _count(m_all)
 
     def send(codes, a, width, dsts, mask, sem):
-        def ap(c0):
-            if codes:
-                return T.gq[:, c0:c0 + width].bitcast(dt.uint8)
-            return T.gs[:, c0:c0 + width]
-        ids = [DstId(rid=topo.addr(d)[0], pnc=topo.addr(d)[1]) for d, _ in dsts]
+        if codes:
+            ap = T.gq[:, a:a + width].bitcast(dt.uint8)
+        else:
+            ap = T.gs[:, a:a + width]
+        ids = [DstId(rid=topo.addr(d)[0], pnc=topo.addr(d)[1]) for d in dsts]
         g.remote_dma_fused([RemoteDMATransfer(dst_ids=ids, dma_engine_mask=mask, remote_sem=sem,
-                                              srcs=[ap(a)], dsts=[ap(c0) for _, c0 in dsts])], local_sem=S.loc)
+                                              srcs=[ap], dsts=[ap for _ in dsts])], local_sem=S.loc)
         return _count(mask)
 
     H = 2 * W * G
@@ -112,28 +127,24 @@ def rank_program(g, core, T, topo):
             vec.wait_ge(S["mv%d" % i], 1)
             vec.tensor_tensor(T.hb[:, i:4 * W:4], T.rl[:, W * i:W * i + W],
                               T.ps[:, BANK * (G + i):BANK * (G + i) + W], AluOpType.mult).then_inc(S.hm, 1)
-    own = slot(here, core)
+    own = col(core)
     vec.wait_ge(S.hm, G)
     vec.quantize_mx(T.gq[:, own:own + W], T.gs[:, own:own + W], T.hb[:]).then_inc(S.qh, 1)
     vec.wait_ge(S.lw, 16)
     vec.quantize_mx(T.wq[:], T.ws[:], T.wb[:]).then_inc(S.qw, 1)
 
+    pair, wide, n_src = pair_of(core)
+    fw = S["fw%d" % mine.index(core)]
     left = 0
     g.wait_ge(S.qh, 1)
-    off = [(d, slot(topo.chip(d), core)) for d in far]
-    left += send(False, own, W, off, m_off, S.offp)
-    left += send(True, own, W, off, m_off, S.offc)
-    near = [(p, own) for p in peers]
-    left += send(True, own, W, near, m_on, S.on)
-    left += send(False, own, W, near, m_on, S.on)
-    pair = slot(here, far[0])
-    assert [slot(here, d) for d in far] == [pair + W * s for s in range(len(far))]
-    wide = W * len(far)
-    on_to = [(p, pair) for p in peers]
-    g.wait_ge(S.offp, n_off * len(far))
-    left += send(False, pair, wide, on_to, m_all, S.fw)
-    g.wait_ge(S.offc, n_off * len(far))
-    left += send(True, pair, wide, on_to, m_all, S.fw)
+    left += send(False, own, W, far, m_off, S.offp)
+    left += send(True, own, W, far, m_off, S.offc)
+    left += send(True, own, W, peers, m_on, S.on)
+    left += send(False, own, W, peers, m_on, S.on)
+    g.wait_ge(S.offp, n_off * n_src)
+    left += send(False, pair, wide, peers, m_all, fw)
+    g.wait_ge(S.offc, n_off * n_src)
+    left += send(True, pair, wide, peers, m_all, fw)
     g.wait_ge(S.loc, left)
 
     def copy(k, out, in_):
@@ -141,48 +152,41 @@ def rank_program(g, core, T, topo):
             return vec.tensor_copy(out, in_)
         return act.activation(out, in_, ActivationFunctionType.Copy)
 
-    def product(bank, col, n, sem):
-        ten.matmul_mx(T.ps[:, BANK * bank:BANK * bank + n], T.wq[:], T.ws[:], T.gq[:, col:col + n],
-                      T.gs[:, col:col + n], True, True).then_inc(sem, 1)
-
-    def ycol(o):
-        return W * T.rank_of(o)
+    def product(bank, c0, n, sem):
+        ten.matmul_mx(T.ps[:, BANK * bank:BANK * bank + n], T.wq[:], T.ws[:], T.gq[:, c0:c0 + n],
+                      T.gs[:, c0:c0 + n], True, True).then_inc(sem, 1)
 
     ten.wait_ge(S.qw, 1)
     ten.wait_ge(S.qh, 1)
     for i in range(G):
         ten.wait_ge(S["rl%d" % i], 1)
     ten.wait_ge(S.hm, G)
-    assert [ycol(o) for o in mine] == [ycol(mine[0]) + W * k for k in range(L)]
+    y0 = col(mine[0])
+    assert [col(o) for o in mine] == [y0 + W * k for k in range(L)]
     ten.wait_ge(S.on, 2 * n_on * len(peers))
     for k in range(2):
-        product(k, 2 * W * k, 2 * W, S["mo%d" % k])
+        a = y0 + 2 * W * k
+        product(k, a, 2 * W, S["mo%d" % k])
         (vec, act)[k].wait_ge(S["mo%d" % k], 1)
-        y0 = ycol(mine[0]) + 2 * W * k
-        copy(k, T.yb[:, y0:y0 + 2 * W], T.ps[:, BANK * k:BANK * k + 2 * W]).then_inc(S.co, 1)
+        copy(k, T.yb[:, a:a + 2 * W], T.ps[:, BANK * k:BANK * k + 2 * W]).then_inc(S.co, 1)
     syn.wait_ge(S.co, 2)
-    y0 = ycol(mine[0])
     syn.dma_start(T.y[:, y0:y0 + L * W], T.yb[:, y0:y0 + L * W]).then_inc(S.st, 16)
-    ten.wait_ge(S.offp, n_off * len(far))
-    ten.wait_ge(S.offc, n_off * len(far))
-    for s, o in enumerate(far):
-        product(2 + s, slot(here, o), W, S["md%d" % s])
-        (vec, act)[s].wait_ge(S["md%d" % s], 1)
-        copy(s, T.yb[:, ycol(o):ycol(o) + W], T.ps[:, BANK * (2 + s):BANK * (2 + s) + W]).then_inc(S["cg%d" % s], 1)
-    ten.wait_ge(S.fw, 2 * n_all * len(peers))
-    ten.wait_ge(S.co, 2)
-    banks = [4, 5, 6, 7, 0, 1]
-    n = 0
-    for s, ch in enumerate(others):
-        for o in members[ch]:
-            if o in far:
-                continue
-            product(banks[n], slot(here, o), W, S["mf%d" % n])
-            (vec, act)[n % 2].wait_ge(S["mf%d" % n], 1)
-            copy(n % 2, T.yb[:, ycol(o):ycol(o) + W],
-                 T.ps[:, BANK * banks[n]:BANK * banks[n] + W]).then_inc(S["cg%d" % s], 1)
-            n += 1
-        y0 = ycol(members[ch][0])
-        syn.wait_ge(S["cg%d" % s], L)
-        syn.dma_start(T.y[:, y0:y0 + L * W], T.yb[:, y0:y0 + L * W]).then_inc(S.st, 16)
-    syn.wait_ge(S.st, 48)
+    stores = 1
+    jobs = [([(S.offp, n_off * n_src), (S.offc, n_off * n_src)], pair)]
+    for p in givers:
+        jobs.append(([(S["fw%d" % mine.index(p)], 2 * n_all)], pair_of(p)[0]))
+    for j, (waits, a) in enumerate(jobs):
+        for sem, n in waits:
+            ten.wait_ge(sem, n)
+        banks = [(2 + 2 * j) % 8, (3 + 2 * j) % 8]
+        if banks[0] < 2:
+            ten.wait_ge(S.co, 2)
+        for k in range(2):
+            product(banks[k], a + W * k, W, S["m%d%d" % (j, k)])
+            (vec, act)[k].wait_ge(S["m%d%d" % (j, k)], 1)
+            copy(k, T.yb[:, a + W * k:a + W * k + W],
+                 T.ps[:, BANK * banks[k]:BANK * banks[k] + W]).then_inc(S["cb%d" % j], 1)
+        syn.wait_ge(S["cb%d" % j], 2)
+        syn.dma_start(T.y[:, a:a + 2 * W], T.yb[:, a:a + 2 * W]).then_inc(S.st, 16)
+        stores += 1
+    syn.wait_ge(S.st, 16 * stores)

@@ -6,6 +6,8 @@ G = 4
 NT = 12
 C = 0.00048828125
 BANK = 512
+UG = [(0, 2), (2, 4)]
+VG = [(0, 1), (1, 2), (2, 3), (3, 4)]
 
 SCRATCH = {
     "xb": ("sbuf", [128, 4 * W], "bfloat16"),
@@ -22,10 +24,10 @@ SCRATCH = {
     "gq": ("sbuf", [128, W * NT], "float8_e4m3fn_x4"), "gs": ("sbuf", [128, W * NT], "uint8"),
     "yb": ("sbuf", [128, W * NT], "float32"),
 }
-SEMAPHORES = (["lx", "lu", "lv0", "lv1", "lw", "qx", "hm", "qh", "qw", "on", "offp", "offc", "loc",
-               "mo0", "mo1", "co", "st"]
-              + ["%s%d" % (n, i) for n in ("qu", "qv", "mu", "mv", "rl", "fw", "cb") for i in range(G)]
-              + ["m%d%d" % (j, k) for j in range(4) for k in range(2)])
+SEMAPHORES = (["lx", "lw", "qx", "hm", "qh", "qw", "on", "offp", "loc", "mo0", "mo1", "co", "ce", "st", "st2", "go"]
+              + ["oc%d" % i for i in range(3)]
+              + ["%s%d" % (n, i) for n in ("lu", "lv", "qu", "qv", "mu", "mv", "rl", "fp", "f0", "f1",
+                                           "m0", "m1", "c1") for i in range(G)])
 
 
 def _count(mask):
@@ -44,37 +46,38 @@ def rank_program(g, core, T, topo):
         if topo.chip(c) not in chips:
             chips.append(topo.chip(c))
     NCH = len(chips)
+    assert NCH == 3
     members = dict((ch, [c for c in cores if topo.chip(c) == ch]) for ch in chips)
-
-    def col(o):
-        return W * T.rank_of(o)
 
     def on_die(ch, d):
         return [c for c in members[ch] if topo.die(c) == d]
 
+    def partner(c, ch):
+        return on_die(ch, topo.die(c))[on_die(topo.chip(c), topo.die(c)).index(c)]
+
     def sources(ch):
         return [chips[(chips.index(ch) - s) % NCH] for s in range(1, NCH)]
 
-    def turn(c):
-        return on_die(topo.chip(c), topo.die(c)).index(c)
+    def col(o):
+        return W * T.rank_of(o)
 
-    here, die = topo.chip(core), topo.die(core)
+    def pcol(o, ch):
+        if topo.chip(o) == ch:
+            return W * members[ch].index(o)
+        return W * (len(members[ch]) + (NCH - 1) * members[ch].index(partner(o, ch)) + sources(ch).index(topo.chip(o)))
+
+    here = topo.chip(core)
+    ci = chips.index(here)
     mine = members[here]
     L = len(mine)
-    far = []
-    for s in range(1, NCH):
-        ch = chips[(chips.index(here) + s) % NCH]
-        far.append(on_die(ch, die)[sources(ch).index(here)])
+    k = mine.index(core)
+    far = [partner(core, chips[(ci + s) % NCH]) for s in range(1, NCH)]
+    back = sources(here)
     for d in far:
-        assert topo.may_write(core, d) and topo.die(d) == die
+        assert topo.may_write(core, d) and topo.die(d) == topo.die(core) and partner(d, here) == core
 
-    def pair_of(c):
-        src = on_die(sources(topo.chip(c))[turn(c)], topo.die(c))
-        assert [col(o) for o in src] == [col(src[0]) + W * k for k in range(len(src))]
-        return col(src[0]), W * len(src), len(src)
-
-    peers = sorted([p for p in mine if p != core], key=lambda p: (turn(p) == turn(core), topo.die(p) != die))
-    givers = sorted([p for p in mine if p != core], key=lambda p: (turn(p), topo.die(p) != die))
+    peers = [mine[(k + s) % L] for s in range(1, L)]
+    givers = [mine[(k - s) % L] for s in range(1, L)]
 
     m_off = topo.mask(core, far[0])
     for d in far:
@@ -83,78 +86,105 @@ def rank_program(g, core, T, topo):
     m_on = m_all & ~m_off
     n_off, n_on, n_all = _count(m_off), _count(m_on), _count(m_all)
 
-    def send(codes, a, width, dsts, mask, sem):
-        if codes:
-            ap = T.gq[:, a:a + width].bitcast(dt.uint8)
-        else:
-            ap = T.gs[:, a:a + width]
-        ids = [DstId(rid=topo.addr(d)[0], pnc=topo.addr(d)[1]) for d in dsts]
-        g.remote_dma_fused([RemoteDMATransfer(dst_ids=ids, dma_engine_mask=mask, remote_sem=sem,
-                                              srcs=[ap], dsts=[ap for _ in dsts])], local_sem=S.loc)
-        return _count(mask)
+    def ids(dsts):
+        return [DstId(rid=topo.addr(d)[0], pnc=topo.addr(d)[1]) for d in dsts]
 
-    H = 2 * W * G
-    syn.dma_start(T.xb[:], T.x[:]).then_inc(S.lx, 16)
-    act.dma_start(T.ub[:], T.u[:]).then_inc(S.lu, 16)
-    syn.dma_start(T.vb[:, 0:H], T.v[:, 0:H]).then_inc(S.lv0, 16)
-    act.dma_start(T.vb[:, H:2 * H], T.v[:, H:2 * H]).then_inc(S.lv1, 16)
+    def codes(o, dsts, mask, sem):
+        ap = T.gq[:, col(o):col(o) + W].bitcast(dt.uint8)
+        return RemoteDMATransfer(dst_ids=ids(dsts), dma_engine_mask=mask, remote_sem=sem, srcs=[ap],
+                                 dsts=[ap for _ in dsts]), _count(mask)
+
+    def planes(o, n, dsts, mask, sem):
+        a = pcol(o, here)
+        return RemoteDMATransfer(dst_ids=ids(dsts), dma_engine_mask=mask, remote_sem=sem, srcs=[T.gs[:, a:a + n * W]],
+                                 dsts=[T.gs[:, pcol(o, topo.chip(d)):pcol(o, topo.chip(d)) + n * W] for d in dsts]
+                                 ), _count(mask)
+
+    left = [0]
+
+    def call(*pieces):
+        g.remote_dma_fused([p[0] for p in pieces], local_sem=S.loc)
+        left[0] += sum(p[1] for p in pieces)
+
+    def tl(i, j=None):
+        return slice(4 * W * i, 4 * W * (i + 1 if j is None else j))
+
+    lu, lv = {}, {}
+    loads = [(T.xb[:], T.x[:], S.lx)]
+    for a, b in UG:
+        loads.append((T.ub[:, tl(a, b)], T.u[:, tl(a, b)], S["lu%d" % a]))
+        for i in range(a, b):
+            lu[i] = S["lu%d" % a]
+    for a, b in VG:
+        loads.append((T.vb[:, tl(a, b)], T.v[:, tl(a, b)], S["lv%d" % a]))
+        for i in range(a, b):
+            lv[i] = S["lv%d" % a]
+    for n, (o, i_, sem) in enumerate(loads):
+        (syn, act)[n % 2].dma_start(o, i_).then_inc(sem, 16)
     syn.dma_start(T.wb[:], T.w2[:]).then_inc(S.lw, 16)
+
+    def cw(i):
+        return slice(W * i, W * i + W)
 
     vec.wait_ge(S.lx, 16)
     vec.quantize_mx(T.xq[:], T.xs[:], T.xb[:]).then_inc(S.qx, 1)
     ten.wait_ge(S.qx, 1)
-    vec.wait_ge(S.lu, 16)
     for i in range(G):
-        vec.quantize_mx(T.uq[:, W * i:W * i + W], T.us[:, W * i:W * i + W],
-                        T.ub[:, 4 * W * i:4 * W * i + 4 * W]).then_inc(S["qu%d" % i], 1)
+        vec.wait_ge(lu[i], 16)
+        vec.quantize_mx(T.uq[:, cw(i)], T.us[:, cw(i)], T.ub[:, tl(i)]).then_inc(S["qu%d" % i], 1)
         ten.wait_ge(S["qu%d" % i], 1)
-        ten.matmul_mx(T.ps[:, BANK * i:BANK * i + W], T.uq[:, W * i:W * i + W], T.us[:, W * i:W * i + W],
+        ten.matmul_mx(T.ps[:, BANK * i:BANK * i + W], T.uq[:, cw(i)], T.us[:, cw(i)],
                       T.xq[:], T.xs[:], True, True).then_inc(S["mu%d" % i], 1)
         act.wait_ge(S["mu%d" % i], 1)
-        act.activation(T.rl[:, W * i:W * i + W], T.ps[:, BANK * i:BANK * i + W], ActivationFunctionType.Relu,
+        act.activation(T.rl[:, cw(i)], T.ps[:, BANK * i:BANK * i + W], ActivationFunctionType.Relu,
                        scale=C).then_inc(S["rl%d" % i], 1)
-    for half in range(2):
-        vec.wait_ge(S["lv%d" % half], 16)
-        two = (2 * half, 2 * half + 1)
-        for i in two:
-            vec.quantize_mx(T.vq[:, W * i:W * i + W], T.vs[:, W * i:W * i + W],
-                            T.vb[:, 4 * W * i:4 * W * i + 4 * W]).then_inc(S["qv%d" % i], 1)
-            ten.wait_ge(S["qv%d" % i], 1)
-            ten.matmul_mx(T.ps[:, BANK * (G + i):BANK * (G + i) + W], T.vq[:, W * i:W * i + W],
-                          T.vs[:, W * i:W * i + W], T.xq[:], T.xs[:], True, True).then_inc(S["mv%d" % i], 1)
-        for i in two:
-            vec.wait_ge(S["rl%d" % i], 1)
-            vec.wait_ge(S["mv%d" % i], 1)
-            vec.tensor_tensor(T.hb[:, i:4 * W:4], T.rl[:, W * i:W * i + W],
-                              T.ps[:, BANK * (G + i):BANK * (G + i) + W], AluOpType.mult).then_inc(S.hm, 1)
-    own = col(core)
+
+    def gate(i):
+        vec.wait_ge(S["rl%d" % i], 1)
+        vec.wait_ge(S["mv%d" % i], 1)
+        vec.tensor_tensor(T.hb[:, i:4 * W:4], T.rl[:, cw(i)],
+                          T.ps[:, BANK * (G + i):BANK * (G + i) + W], AluOpType.mult).then_inc(S.hm, 1)
+
+    for i in range(G):
+        vec.wait_ge(lv[i], 16)
+        vec.quantize_mx(T.vq[:, cw(i)], T.vs[:, cw(i)], T.vb[:, tl(i)]).then_inc(S["qv%d" % i], 1)
+        ten.wait_ge(S["qv%d" % i], 1)
+        ten.matmul_mx(T.ps[:, BANK * (G + i):BANK * (G + i) + W], T.vq[:, cw(i)], T.vs[:, cw(i)],
+                      T.xq[:], T.xs[:], True, True).then_inc(S["mv%d" % i], 1)
+        if i > 0:
+            gate(i - 1)
+    gate(G - 1)
     vec.wait_ge(S.hm, G)
-    vec.quantize_mx(T.gq[:, own:own + W], T.gs[:, own:own + W], T.hb[:]).then_inc(S.qh, 1)
+    vec.quantize_mx(T.gq[:, col(core):col(core) + W], T.gs[:, pcol(core, here):pcol(core, here) + W],
+                    T.hb[:]).then_inc(S.qh, 1)
     vec.wait_ge(S.lw, 16)
     vec.quantize_mx(T.wq[:], T.ws[:], T.wb[:]).then_inc(S.qw, 1)
 
-    pair, wide, n_src = pair_of(core)
-    fw = S["fw%d" % mine.index(core)]
-    left = 0
+    got = [partner(core, ch) for ch in back]
+    oc = [S["oc%d" % chips.index(ch)] for ch in back]
+    assert pcol(got[1], here) == pcol(got[0], here) + W
     g.wait_ge(S.qh, 1)
-    left += send(False, own, W, far, m_off, S.offp)
-    left += send(True, own, W, far, m_off, S.offc)
-    left += send(True, own, W, peers, m_on, S.on)
-    left += send(False, own, W, peers, m_on, S.on)
-    g.wait_ge(S.offp, n_off * n_src)
-    left += send(False, pair, wide, peers, m_all, fw)
-    g.wait_ge(S.offc, n_off * n_src)
-    left += send(True, pair, wide, peers, m_all, fw)
-    g.wait_ge(S.loc, left)
+    call(planes(core, 1, far, m_off, S.offp))
+    call(codes(core, far, m_off, S["oc%d" % ci]))
+    call(codes(core, peers, m_on, S.on))
+    call(planes(core, 1, peers[:1], m_off, S.on), planes(core, 1, peers[1:], m_on, S.on))
+    g.wait_ge(S.offp, n_off * len(back))
+    call(planes(got[0], 2, peers, m_all, S["fp%d" % k]))
+    for s in range(2):
+        g.wait_ge(oc[s], n_off)
+        call(codes(got[s], peers, m_all, S["f%d%d" % (s, k)]))
+    g.sem_inc(S.go, 1)
+    g.wait_ge(S.loc, left[0])
 
-    def copy(k, out, in_):
-        if k == 0:
+    def copy(e, out, in_):
+        if e == 0:
             return vec.tensor_copy(out, in_)
         return act.activation(out, in_, ActivationFunctionType.Copy)
 
-    def product(bank, c0, n, sem):
-        ten.matmul_mx(T.ps[:, BANK * bank:BANK * bank + n], T.wq[:], T.ws[:], T.gq[:, c0:c0 + n],
-                      T.gs[:, c0:c0 + n], True, True).then_inc(sem, 1)
+    def product(bank, o, n, sem):
+        a, b = col(o), pcol(o, here)
+        ten.matmul_mx(T.ps[:, BANK * bank:BANK * bank + n * W], T.wq[:], T.ws[:], T.gq[:, a:a + n * W],
+                      T.gs[:, b:b + n * W], True, True).then_inc(sem, 1)
 
     ten.wait_ge(S.qw, 1)
     ten.wait_ge(S.qh, 1)
@@ -162,31 +192,51 @@ def rank_program(g, core, T, topo):
         ten.wait_ge(S["rl%d" % i], 1)
     ten.wait_ge(S.hm, G)
     y0 = col(mine[0])
-    assert [col(o) for o in mine] == [y0 + W * k for k in range(L)]
-    ten.wait_ge(S.on, 2 * n_on * len(peers))
-    for k in range(2):
-        a = y0 + 2 * W * k
-        product(k, a, 2 * W, S["mo%d" % k])
-        (vec, act)[k].wait_ge(S["mo%d" % k], 1)
-        copy(k, T.yb[:, a:a + 2 * W], T.ps[:, BANK * k:BANK * k + 2 * W]).then_inc(S.co, 1)
+    assert [col(o) for o in mine] == [y0 + W * j for j in range(L)]
+    ten.wait_ge(S.on, n_on * len(givers) + n_off + n_on * (len(givers) - 1))
+    for e in range(2):
+        a = y0 + 2 * W * e
+        product(e, mine[2 * e], 2, S["mo%d" % e])
+        (vec, act)[e].wait_ge(S["mo%d" % e], 1)
+        copy(e, T.yb[:, a:a + 2 * W], T.ps[:, BANK * e:BANK * e + 2 * W]).then_inc(S.co, 1)
     syn.wait_ge(S.co, 2)
+    syn.wait_ge(S.go, 1)
     syn.dma_start(T.y[:, y0:y0 + L * W], T.yb[:, y0:y0 + L * W]).then_inc(S.st, 16)
-    stores = 1
-    jobs = [([(S.offp, n_off * n_src), (S.offc, n_off * n_src)], pair)]
-    for p in givers:
-        jobs.append(([(S["fw%d" % mine.index(p)], 2 * n_all)], pair_of(p)[0]))
-    for j, (waits, a) in enumerate(jobs):
-        for sem, n in waits:
-            ten.wait_ge(sem, n)
-        banks = [(2 + 2 * j) % 8, (3 + 2 * j) % 8]
-        if banks[0] < 2:
-            ten.wait_ge(S.co, 2)
-        for k in range(2):
-            product(banks[k], a + W * k, W, S["m%d%d" % (j, k)])
-            (vec, act)[k].wait_ge(S["m%d%d" % (j, k)], 1)
-            copy(k, T.yb[:, a + W * k:a + W * k + W],
-                 T.ps[:, BANK * banks[k]:BANK * banks[k] + W]).then_inc(S["cb%d" % j], 1)
-        syn.wait_ge(S["cb%d" % j], 2)
-        syn.dma_start(T.y[:, a:a + 2 * W], T.yb[:, a:a + 2 * W]).then_inc(S.st, 16)
-        stores += 1
-    syn.wait_ge(S.st, 16 * stores)
+    n_syn, n_act = 1, 0
+    for s in range(2):
+        ch = back[s]
+        for j, p in enumerate([core] + givers):
+            o = partner(p, ch)
+            a = col(o)
+            if p == core:
+                ten.wait_ge(S.offp, n_off * len(back))
+                ten.wait_ge(oc[s], n_off)
+            else:
+                ten.wait_ge(S["fp%d" % mine.index(p)], n_all)
+                ten.wait_ge(S["f%d%d" % (s, mine.index(p))], n_all)
+            bank = (2 + 4 * s + j) % 8
+            if bank < 2:
+                ten.wait_ge(S.co, 2)
+            product(bank, o, 1, S["m%d%d" % (s, j)])
+            e = j % 2 if s == 0 else 0
+            (vec, act)[e].wait_ge(S["m%d%d" % (s, j)], 1)
+            done = copy(e, T.yb[:, a:a + W], T.ps[:, BANK * bank:BANK * bank + W])
+            if s == 0:
+                done.then_inc(S.ce, 1)
+            else:
+                done.then_inc(S["c1%d" % j], 1)
+                if j in (1, 2):
+                    act.wait_ge(S["c1%d" % j], 1)
+                    act.dma_start(T.y[:, a:a + W], T.yb[:, a:a + W]).then_inc(S.st2, 16)
+                    n_act += 1
+                else:
+                    syn.wait_ge(S["c1%d" % j], 1)
+                    syn.dma_start(T.y[:, a:a + W], T.yb[:, a:a + W]).then_inc(S.st, 16)
+                    n_syn += 1
+        if s == 0:
+            b0 = col(members[ch][0])
+            syn.wait_ge(S.ce, L)
+            syn.dma_start(T.y[:, b0:b0 + L * W], T.yb[:, b0:b0 + L * W]).then_inc(S.st, 16)
+            n_syn += 1
+    syn.wait_ge(S.st, 16 * n_syn)
+    act.wait_ge(S.st2, 16 * n_act)

from concourse.bass import DstId, RemoteDMATransfer
from concourse.mybir import dt, AluOpType, ActivationFunctionType

W = 128
G = 4
NT = 12
C = 0.00048828125
BANK = 512
UG = [(0, 2), (2, 4)]
VG = [(0, 1), (1, 2), (2, 3), (3, 4)]

SCRATCH = {
    "xb": ("sbuf", [128, 4 * W], "bfloat16"),
    "ub": ("sbuf", [128, 4 * W * G], "bfloat16"),
    "vb": ("sbuf", [128, 4 * W * G], "bfloat16"),
    "wb": ("sbuf", [128, 4 * W], "bfloat16"),
    "xq": ("sbuf", [128, W], "float8_e4m3fn_x4"), "xs": ("sbuf", [128, W], "uint8"),
    "uq": ("sbuf", [128, W * G], "float8_e4m3fn_x4"), "us": ("sbuf", [128, W * G], "uint8"),
    "vq": ("sbuf", [128, W * G], "float8_e4m3fn_x4"), "vs": ("sbuf", [128, W * G], "uint8"),
    "wq": ("sbuf", [128, W], "float8_e4m3fn_x4"), "ws": ("sbuf", [128, W], "uint8"),
    "ps": ("psum", [128, 8 * BANK], "float32"),
    "rl": ("sbuf", [128, W * G], "float32"),
    "hb": ("sbuf", [128, 4 * W], "bfloat16"),
    "gq": ("sbuf", [128, W * NT], "float8_e4m3fn_x4"), "gs": ("sbuf", [128, W * NT], "uint8"),
    "yb": ("sbuf", [128, W * NT], "float32"),
}
SEMAPHORES = (["lx", "lw", "qx", "hm", "qh", "qw", "on", "offp", "loc", "mo0", "mo1", "co", "ce", "st", "st2", "go"]
              + ["oc%d" % i for i in range(3)]
              + ["%s%d" % (n, i) for n in ("lu", "lv", "qu", "qv", "mu", "mv", "rl", "fp", "f0", "f1",
                                           "m0", "m1", "c1") for i in range(G)])


def _count(mask):
    return bin(mask).count("1")


def rank_program(g, core, T, topo):
    if T.rank_of(core) is None:
        return
    S = T.sem
    vec, ten, act, syn = g.vector, g.tensor, g.scalar, g.sync

    cores = list(T.cores)
    chips = []
    for c in cores:
        if topo.chip(c) not in chips:
            chips.append(topo.chip(c))
    NCH = len(chips)
    assert NCH == 3
    members = dict((ch, [c for c in cores if topo.chip(c) == ch]) for ch in chips)

    def on_die(ch, d):
        return [c for c in members[ch] if topo.die(c) == d]

    def partner(c, ch):
        return on_die(ch, topo.die(c))[on_die(topo.chip(c), topo.die(c)).index(c)]

    def sources(ch):
        return [chips[(chips.index(ch) - s) % NCH] for s in range(1, NCH)]

    def col(o):
        return W * T.rank_of(o)

    def pcol(o, ch):
        if topo.chip(o) == ch:
            return W * members[ch].index(o)
        return W * (len(members[ch]) + (NCH - 1) * members[ch].index(partner(o, ch)) + sources(ch).index(topo.chip(o)))

    here = topo.chip(core)
    ci = chips.index(here)
    mine = members[here]
    L = len(mine)
    k = mine.index(core)
    far = [partner(core, chips[(ci + s) % NCH]) for s in range(1, NCH)]
    back = sources(here)
    for d in far:
        assert topo.may_write(core, d) and topo.die(d) == topo.die(core) and partner(d, here) == core

    peers = [mine[(k + s) % L] for s in range(1, L)]
    givers = [mine[(k - s) % L] for s in range(1, L)]

    m_off = topo.mask(core, far[0])
    for d in far:
        m_off &= topo.mask(core, d)
    m_all = topo.mask(core, peers[0])
    m_on = m_all & ~m_off
    n_off, n_on, n_all = _count(m_off), _count(m_on), _count(m_all)

    def ids(dsts):
        return [DstId(rid=topo.addr(d)[0], pnc=topo.addr(d)[1]) for d in dsts]

    def codes(o, dsts, mask, sem):
        ap = T.gq[:, col(o):col(o) + W].bitcast(dt.uint8)
        return RemoteDMATransfer(dst_ids=ids(dsts), dma_engine_mask=mask, remote_sem=sem, srcs=[ap],
                                 dsts=[ap for _ in dsts]), _count(mask)

    def planes(o, n, dsts, mask, sem):
        a = pcol(o, here)
        return RemoteDMATransfer(dst_ids=ids(dsts), dma_engine_mask=mask, remote_sem=sem, srcs=[T.gs[:, a:a + n * W]],
                                 dsts=[T.gs[:, pcol(o, topo.chip(d)):pcol(o, topo.chip(d)) + n * W] for d in dsts]
                                 ), _count(mask)

    left = [0]

    def call(*pieces):
        g.remote_dma_fused([p[0] for p in pieces], local_sem=S.loc)
        left[0] += sum(p[1] for p in pieces)

    def tl(i, j=None):
        return slice(4 * W * i, 4 * W * (i + 1 if j is None else j))

    lu, lv = {}, {}
    loads = [(T.xb[:], T.x[:], S.lx)]
    for a, b in UG:
        loads.append((T.ub[:, tl(a, b)], T.u[:, tl(a, b)], S["lu%d" % a]))
        for i in range(a, b):
            lu[i] = S["lu%d" % a]
    for a, b in VG:
        loads.append((T.vb[:, tl(a, b)], T.v[:, tl(a, b)], S["lv%d" % a]))
        for i in range(a, b):
            lv[i] = S["lv%d" % a]
    for n, (o, i_, sem) in enumerate(loads):
        (syn, act)[n % 2].dma_start(o, i_).then_inc(sem, 16)
    syn.dma_start(T.wb[:], T.w2[:]).then_inc(S.lw, 16)

    def cw(i):
        return slice(W * i, W * i + W)

    vec.wait_ge(S.lx, 16)
    vec.quantize_mx(T.xq[:], T.xs[:], T.xb[:]).then_inc(S.qx, 1)
    ten.wait_ge(S.qx, 1)
    for i in range(G):
        vec.wait_ge(lu[i], 16)
        vec.quantize_mx(T.uq[:, cw(i)], T.us[:, cw(i)], T.ub[:, tl(i)]).then_inc(S["qu%d" % i], 1)
        ten.wait_ge(S["qu%d" % i], 1)
        ten.matmul_mx(T.ps[:, BANK * i:BANK * i + W], T.uq[:, cw(i)], T.us[:, cw(i)],
                      T.xq[:], T.xs[:], True, True).then_inc(S["mu%d" % i], 1)
        act.wait_ge(S["mu%d" % i], 1)
        act.activation(T.rl[:, cw(i)], T.ps[:, BANK * i:BANK * i + W], ActivationFunctionType.Relu,
                       scale=C).then_inc(S["rl%d" % i], 1)

    def gate(i):
        vec.wait_ge(S["rl%d" % i], 1)
        vec.wait_ge(S["mv%d" % i], 1)
        vec.tensor_tensor(T.hb[:, i:4 * W:4], T.rl[:, cw(i)],
                          T.ps[:, BANK * (G + i):BANK * (G + i) + W], AluOpType.mult).then_inc(S.hm, 1)

    for i in range(G):
        vec.wait_ge(lv[i], 16)
        vec.quantize_mx(T.vq[:, cw(i)], T.vs[:, cw(i)], T.vb[:, tl(i)]).then_inc(S["qv%d" % i], 1)
        ten.wait_ge(S["qv%d" % i], 1)
        ten.matmul_mx(T.ps[:, BANK * (G + i):BANK * (G + i) + W], T.vq[:, cw(i)], T.vs[:, cw(i)],
                      T.xq[:], T.xs[:], True, True).then_inc(S["mv%d" % i], 1)
        if i > 0:
            gate(i - 1)
    gate(G - 1)
    vec.wait_ge(S.hm, G)
    vec.quantize_mx(T.gq[:, col(core):col(core) + W], T.gs[:, pcol(core, here):pcol(core, here) + W],
                    T.hb[:]).then_inc(S.qh, 1)
    vec.wait_ge(S.lw, 16)
    vec.quantize_mx(T.wq[:], T.ws[:], T.wb[:]).then_inc(S.qw, 1)

    got = [partner(core, ch) for ch in back]
    oc = [S["oc%d" % chips.index(ch)] for ch in back]
    assert pcol(got[1], here) == pcol(got[0], here) + W
    g.wait_ge(S.qh, 1)
    call(planes(core, 1, far, m_off, S.offp))
    call(codes(core, far, m_off, S["oc%d" % ci]))
    call(codes(core, peers, m_on, S.on))
    call(planes(core, 1, peers[:1], m_off, S.on), planes(core, 1, peers[1:], m_on, S.on))
    g.wait_ge(S.offp, n_off * len(back))
    call(planes(got[0], 2, peers, m_all, S["fp%d" % k]))
    for s in range(2):
        g.wait_ge(oc[s], n_off)
        call(codes(got[s], peers, m_all, S["f%d%d" % (s, k)]))
    g.sem_inc(S.go, 1)
    g.wait_ge(S.loc, left[0])

    def copy(e, out, in_):
        if e == 0:
            return vec.tensor_copy(out, in_)
        return act.activation(out, in_, ActivationFunctionType.Copy)

    def product(bank, o, n, sem):
        a, b = col(o), pcol(o, here)
        ten.matmul_mx(T.ps[:, BANK * bank:BANK * bank + n * W], T.wq[:], T.ws[:], T.gq[:, a:a + n * W],
                      T.gs[:, b:b + n * W], True, True).then_inc(sem, 1)

    ten.wait_ge(S.qw, 1)
    ten.wait_ge(S.qh, 1)
    for i in range(G):
        ten.wait_ge(S["rl%d" % i], 1)
    ten.wait_ge(S.hm, G)
    y0 = col(mine[0])
    assert [col(o) for o in mine] == [y0 + W * j for j in range(L)]
    ten.wait_ge(S.on, n_on * len(givers) + n_off + n_on * (len(givers) - 1))
    for e in range(2):
        a = y0 + 2 * W * e
        product(e, mine[2 * e], 2, S["mo%d" % e])
        (vec, act)[e].wait_ge(S["mo%d" % e], 1)
        copy(e, T.yb[:, a:a + 2 * W], T.ps[:, BANK * e:BANK * e + 2 * W]).then_inc(S.co, 1)
    syn.wait_ge(S.co, 2)
    syn.wait_ge(S.go, 1)
    syn.dma_start(T.y[:, y0:y0 + L * W], T.yb[:, y0:y0 + L * W]).then_inc(S.st, 16)
    n_syn, n_act = 1, 0
    for s in range(2):
        ch = back[s]
        for j, p in enumerate([core] + givers):
            o = partner(p, ch)
            a = col(o)
            if p == core:
                ten.wait_ge(S.offp, n_off * len(back))
                ten.wait_ge(oc[s], n_off)
            else:
                ten.wait_ge(S["fp%d" % mine.index(p)], n_all)
                ten.wait_ge(S["f%d%d" % (s, mine.index(p))], n_all)
            bank = (2 + 4 * s + j) % 8
            if bank < 2:
                ten.wait_ge(S.co, 2)
            product(bank, o, 1, S["m%d%d" % (s, j)])
            e = j % 2 if s == 0 else 0
            (vec, act)[e].wait_ge(S["m%d%d" % (s, j)], 1)
            done = copy(e, T.yb[:, a:a + W], T.ps[:, BANK * bank:BANK * bank + W])
            if s == 0:
                done.then_inc(S.ce, 1)
            else:
                done.then_inc(S["c1%d" % j], 1)
                if j in (1, 2):
                    act.wait_ge(S["c1%d" % j], 1)
                    act.dma_start(T.y[:, a:a + W], T.yb[:, a:a + W]).then_inc(S.st2, 16)
                    n_act += 1
                else:
                    syn.wait_ge(S["c1%d" % j], 1)
                    syn.dma_start(T.y[:, a:a + W], T.yb[:, a:a + W]).then_inc(S.st, 16)
                    n_syn += 1
        if s == 0:
            b0 = col(members[ch][0])
            syn.wait_ge(S.ce, L)
            syn.dma_start(T.y[:, b0:b0 + L * W], T.yb[:, b0:b0 + L * W]).then_inc(S.st, 16)
            n_syn += 1
    syn.wait_ge(S.st, 16 * n_syn)
    act.wait_ge(S.st2, 16 * n_act)
